import numpy as np
import ml_dtypes


def mxq(x, axis, fmt="e4m3"):
    dtype, down = {"e4m3": (ml_dtypes.float8_e4m3fn, 7), "e5m2": (ml_dtypes.float8_e5m2, 14)}[fmt]
    v = np.moveaxis(np.asarray(x, np.float32).astype(ml_dtypes.bfloat16).astype(np.float64), axis, -1)
    blocks = v.reshape(v.shape[:-1] + (-1, 32))
    amax = np.abs(blocks).max(-1, keepdims=True)
    byte = np.maximum(np.where(amax > 0, np.frexp(amax)[1] - 1 + 127, 0) - down, 1)
    scale = np.exp2(byte - 127.0)
    codes = (blocks / scale).astype(np.float32).astype(dtype).astype(np.float64)
    return np.moveaxis((codes * scale).reshape(v.shape), -1, axis)


WIDE = False


def mx_kscale(k):
    if not WIDE:
        return np.ones(k)
    levels = np.array([10, -10, 5, -5, 0])
    if k % 512:
        return np.exp2(np.random.permutation(np.resize(levels, k // 32))).repeat(32)
    a = np.empty((k // 512, 16))
    for p in range(k // 512):
        a[p, :8] = np.random.permutation(np.resize(levels, 8))
        for g in range(8):
            far = levels[np.abs(levels - a[p, g]) >= 10]
            a[p, g + 8] = far[np.random.randint(len(far))]
    return np.exp2(a.ravel()).repeat(32)


def f64(x):
    return np.asarray(x).astype(np.float64)


def striped(idx):
    return np.tile(idx.reshape(-1, 16).T, (8, 1)).astype(np.uint16)


def unstriped(offs):
    return offs[:16].T.reshape(-1).astype(np.int64)


def pack_weight(w):
    k, n = w.shape
    w = f64(np.asarray(w, np.float32).astype(ml_dtypes.bfloat16)).reshape(k // 32, 32, n)
    amax = np.abs(w).max(1)
    byte = np.clip(np.where(amax > 0, np.frexp(amax)[1] - 1 + 127 - 7, 1), 1, 254)
    scaled = (w * np.exp2(127.0 - byte)[:, None, :]).reshape(k, n).astype(np.float32)
    words = np.ascontiguousarray(scaled.reshape(k // 512, 128, 4, n).transpose(0, 1, 3, 2)).astype(ml_dtypes.float8_e4m3fn).view(np.uint8)
    return words, np.ascontiguousarray(byte.astype(np.uint8).reshape(k // 512, 16, n))


def unpack_weight(words, scales):
    g, p, n, _ = words.shape
    vals = np.ascontiguousarray(words).view(ml_dtypes.float8_e4m3fn).astype(np.float64) * np.repeat(np.exp2(scales.astype(np.float64) - 127.0), 8, axis=1)[..., None]
    return vals.transpose(0, 1, 3, 2).reshape(g * 512, n)


K, T, S, D, N = 512, 2048, 1024, 4, 256
P = 2 ** 7


def setup_inputs():
    n = np.random.standard_normal
    s = mx_kscale(K)[:, None]
    packed_xT = pack_weight(n((K, T)) * s)
    return {
        "x_words": packed_xT[0],
        "x_scales": packed_xT[1],
        "w1": (n((K, N)) / np.sqrt(K) / s).astype(np.float32),
        "apo": (np.tile(np.random.uniform(0.3, 1.0, S), (P, 1))).astype(np.float32),
        "offs": striped(np.random.permutation(T)[:S]),
    }


def reference(x_words, x_scales, w1, apo, offs):
    xq = unpack_weight(x_words, x_scales)[:, unstriped(offs)]
    y = mxq(f64(w1), 0, "e4m3").T @ xq
    ys = y * f64(apo)[:1]
    beam = ys.reshape(len(ys), -1, D).sum(axis=2)
    y2 = (y) ** 2
    co = ((y.reshape(len(y), -1, D).sum(axis=2)) ** 2) / (4.0 * (y2.reshape(len(y2), -1, D).sum(axis=2)) + 0.1)
    return beam * co

@@ -1,0 +1,171 @@
+from contextlib import ExitStack
+
+import concourse.mybir as mybir
+from concourse.masks import make_identity
+
+K, T, S, D, N = 512, 2048, 1024, 4, 256
+P = 128
+PACK = 4
+HALVES = S // (D * P)
+FLOPS = 2 * K * N * S
+BYTES = K * T + 16 * T + 4 * K * N + 4 * S + 2 * P * (S // 16) + 4 * N * (S // D)
+
+F32 = mybir.dt.float32
+BF16 = mybir.dt.bfloat16
+I32 = mybir.dt.int32
+U32 = mybir.dt.uint32
+U16 = mybir.dt.uint16
+U8 = mybir.dt.uint8
+FP8X4 = mybir.dt.float8_e4m3fn_x4
+ACT = mybir.ActivationFunctionType
+ALU = mybir.AluOpType
+
+
+def tile_picked_ydas_lin_p_kernel(tc, x_words, x_scales, w1, apo, offs, out):
+    nc = tc.nc
+    with ExitStack() as ctx:
+        keep = ctx.enter_context(tc.tile_pool(name="keep", bufs=1))
+        psum = ctx.enter_context(tc.psum_pool(name="psum", bufs=1))
+
+        offsets = keep.tile([P, S // 16], U16, name="offsets")
+        nc.sync.dma_start(offsets[:], offs)
+
+        gain = keep.tile([P, HALVES, D], F32, name="gain")
+        nc.sync.dma_start(gain[:], apo[0, :].rearrange("(h v d) -> v h d", h=HALVES, d=D))
+
+        scale_table = keep.tile([P, T], U8, name="scale_table", align_bytes=64)
+        nc.vector.memset(scale_table[:].bitcast(I32), 0)
+        for q in range(4):
+            nc.sync.dma_start(
+                scale_table[32 * q : 32 * q + 4, :].bitcast(I32),
+                x_scales[0, 4 * q : 4 * q + 4, :].bitcast(I32),
+            )
+        warm_in = keep.tile([P, 1], F32, name="warm_in")
+        warm_out = keep.tile([P, 1], F32, name="warm_out")
+        nc.vector.memset(warm_in[:], 1.0)
+        nc.scalar.activation(warm_out[:], warm_in[:], ACT.Abs_reciprocal_sqrt)
+
+        w_raw = keep.tile([P, PACK, N], F32, name="w_raw")
+        nc.sync.dma_start(w_raw[:], w1.rearrange("(p j) n -> p j n", j=PACK))
+        word_table = keep.tile([P, T], U32, name="word_table", align_bytes=64)
+        nc.sync.dma_start(word_table[:].bitcast(I32), x_words[0].rearrange("p n t -> p (n t)").bitcast(I32))
+
+        identity = keep.tile([P, P], F32, name="identity")
+        make_identity(nc, identity[:])
+
+        listed_scales = keep.tile([P, S], U8, name="listed_scales", align_bytes=64)
+        nc.vector.tensor_copy(listed_scales[:], scale_table[:].indirect(offsets[:]))
+        x_scale = keep.tile([P, HALVES, D, P], U8, name="x_scale", align_bytes=64)
+        nc.vector.tensor_copy(x_scale[:], listed_scales[:].rearrange("p (h v d) -> p h d v", h=HALVES, d=D))
+
+        w_grouped = keep.tile([P, N, PACK], BF16, name="w_grouped", align_bytes=64)
+        nc.scalar.copy(w_grouped[:], w_raw[:].rearrange("p j n -> p n j"))
+        w_codes = keep.tile([P, N], U32, name="w_codes", align_bytes=64)
+        w_scale = keep.tile([P, N], U8, name="w_scale", align_bytes=64)
+        nc.vector.quantize_mx(w_codes[:].bitcast(FP8X4), w_scale[:], w_grouped[:].rearrange("p n j -> p (n j)"))
+
+        y = []
+        for h in range(HALVES):
+            x_codes = keep.tile([P, D, P], U32, name=f"x_codes{h}", align_bytes=64)
+            nc.vector.tensor_copy(
+                x_codes[:].rearrange("p d v -> p v d"),
+                word_table[:].indirect(offsets[:, 32 * h : 32 * (h + 1)]),
+            )
+            banks = [psum.tile([P, 2, N], F32, name=f"y{h}{b}", tag=f"bank{h}{b}") for b in range(2)]
+            for d in range(D):
+                nc.tensor.matmul_mx(
+                    banks[d // 2][:, d % 2, :],
+                    lhsT=x_codes[:, d, :].bitcast(FP8X4),
+                    lhsT_scale=x_scale[:, h, d, :],
+                    rhs=w_codes[:].bitcast(FP8X4),
+                    rhs_scale=w_scale[:],
+                    start=True,
+                    stop=True,
+                )
+            y.append(banks)
+
+        total = [[keep.tile([P, N], F32, name=f"total{h}{i}") for i in range(D)] for h in range(HALVES)]
+        beam = [[keep.tile([P, N], F32, name=f"beam{h}{i}") for i in range(D)] for h in range(HALVES)]
+        squares = [[keep.tile([P, 2, N], F32, name=f"squares{h}{b}") for b in range(2)] for h in range(HALVES)]
+        power_t = [psum.tile([P, 2, P], F32, name=f"power_t{h}") for h in range(HALVES)]
+        total_t = [psum.tile([P, 2, P], F32, name="total_t0")]
+        beam_t = [psum.tile([P, 2, P], F32, name="beam_t0")]
+        root = [keep.tile([P, 2, P], F32, name=f"root{h}") for h in range(HALVES)]
+        ratio = [keep.tile([P, 2, P], F32, name=f"ratio{h}") for h in range(HALVES)]
+        coherence = [keep.tile([P, 2, P], F32, name=f"coherence{h}") for h in range(HALVES)]
+        result = [keep.tile([P, 2, P], F32, name=f"result{h}") for h in range(HALVES)]
+
+        def channel(h, d):
+            return y[h][d // 2][:, d % 2, :]
+
+        def open_sums(h):
+            nc.scalar.activation(total[h][0][:], channel(h, 0), ACT.Copy)
+            nc.scalar.activation(beam[h][0][:], channel(h, 0), ACT.Copy, scale=gain[:, h, 0:1])
+
+        def add_total(h, i, d):
+            nc.vector.tensor_tensor(total[h][i + 1][:], channel(h, d), total[h][i][:], ALU.add)
+
+        def add_beam(h, i, d):
+            nc.vector.scalar_tensor_tensor(
+                beam[h][i + 1][:], channel(h, d), gain[:, h, d : d + 1], beam[h][i][:], ALU.mult, ALU.add
+            )
+
+        def square(h, b):
+            nc.scalar.activation(squares[h][b][:], y[h][b][:], ACT.Square)
+
+        def turn_squares(h, order):
+            for mh in range(2):
+                for i, d in enumerate(order):
+                    nc.tensor.matmul(
+                        power_t[h][:, mh, :], squares[h][d // 2][:, d % 2, mh * P : (mh + 1) * P], identity[:],
+                        start=(i == 0), stop=(i == D - 1), is_transpose=True,
+                    )
+
+        def turn(dst, src):
+            for mh in range(2):
+                nc.tensor.transpose(dst[:, mh, :], src[:, mh * P : (mh + 1) * P], identity[:])
+
+        def find_root(h):
+            nc.scalar.activation(root[h][:], power_t[h][:], ACT.Abs_reciprocal_sqrt, bias=0.1, scale=4.0)
+
+        def find_ratio(h):
+            nc.vector.tensor_tensor(ratio[h][:], total_t[h][:], root[h][:], ALU.mult)
+
+        def find_coherence(h):
+            nc.scalar.activation(coherence[h][:], ratio[h][:], ACT.Square)
+
+        def finish(h):
+            nc.vector.tensor_tensor(result[h][:], beam_t[h][:], coherence[h][:], ALU.mult)
+            nc.sync.dma_start(out[:, h * P : (h + 1) * P].rearrange("(mh p) v -> p mh v", p=P), result[h][:])
+
+        open_sums(0)
+        square(0, 0)
+        for i, d in enumerate((2, 3, 1)):
+            add_total(0, i, d)
+            add_beam(0, i, d)
+        open_sums(1)
+        square(1, 1)
+        square(0, 1)
+        turn(total_t[0], total[0][3])
+        turn(beam_t[0], beam[0][3])
+        turn_squares(0, (0, 1, 2, 3))
+        total_t.append(psum.tile([P, 2, P], F32, name="total_t1", tag="bank00"))
+        beam_t.append(psum.tile([P, 2, P], F32, name="beam_t1", tag="bank01"))
+        add_total(1, 0, 1)
+        add_beam(1, 0, 1)
+        square(1, 0)
+        find_root(0)
+        add_total(1, 1, 2)
+        turn_squares(1, (2, 3, 0, 1))
+        find_ratio(0)
+        add_total(1, 2, 3)
+        find_root(1)
+        find_coherence(0)
+        turn(total_t[1], total[1][3])
+        add_beam(1, 1, 2)
+        finish(0)
+        find_ratio(1)
+        add_beam(1, 2, 3)
+        find_coherence(1)
+        turn(beam_t[1], beam[1][3])
+        finish(1)

@@ -30,142 +30,167 @@ def tile_picked_ydas_lin_p_kernel(tc, x_words, x_scales, w1, apo, offs, out):
         offsets = keep.tile([P, S // 16], U16, name="offsets")
         nc.sync.dma_start(offsets[:], offs)
 
-        gain = keep.tile([P, HALVES, D], F32, name="gain")
-        nc.sync.dma_start(gain[:], apo[0, :].rearrange("(h v d) -> v h d", h=HALVES, d=D))
+        w_rows = w1.rearrange("(p j) n -> p j n", j=PACK)
+        w_raw = [keep.tile([P, PACK, P], F32, name=f"w_raw{mh}") for mh in range(2)]
+        nc.sync.dma_start(w_raw[0][:], w_rows[:, :, :P])
 
         scale_table = keep.tile([P, T], U8, name="scale_table", align_bytes=64)
         nc.vector.memset(scale_table[:].bitcast(I32), 0)
-        for q in range(4):
-            nc.sync.dma_start(
-                scale_table[32 * q : 32 * q + 4, :].bitcast(I32),
-                x_scales[0, 4 * q : 4 * q + 4, :].bitcast(I32),
-            )
+        for r in range(4):
+            (nc.sync, nc.scalar)[r % 2].dma_start(scale_table[r:P:32, :].bitcast(I32), x_scales[0, r:16:4, :].bitcast(I32))
         warm_in = keep.tile([P, 1], F32, name="warm_in")
         warm_out = keep.tile([P, 1], F32, name="warm_out")
         nc.vector.memset(warm_in[:], 1.0)
         nc.scalar.activation(warm_out[:], warm_in[:], ACT.Abs_reciprocal_sqrt)
 
-        w_raw = keep.tile([P, PACK, N], F32, name="w_raw")
-        nc.sync.dma_start(w_raw[:], w1.rearrange("(p j) n -> p j n", j=PACK))
+        nc.sync.dma_start(w_raw[1][:], w_rows[:, :, P:])
         word_table = keep.tile([P, T], U32, name="word_table", align_bytes=64)
         nc.sync.dma_start(word_table[:].bitcast(I32), x_words[0].rearrange("p n t -> p (n t)").bitcast(I32))
+        gain = keep.tile([P, HALVES, D], F32, name="gain")
+        nc.sync.dma_start(gain[:], apo[0, :].rearrange("(h v d) -> v h d", h=HALVES, d=D))
 
         identity = keep.tile([P, P], F32, name="identity")
-        make_identity(nc, identity[:])
+        nc.vector.memset(identity[:], 0.0)
+        make_identity(nc, identity[:], nomemset=True)
 
-        listed_scales = keep.tile([P, S], U8, name="listed_scales", align_bytes=64)
-        nc.vector.tensor_copy(listed_scales[:], scale_table[:].indirect(offsets[:]))
-        x_scale = keep.tile([P, HALVES, D, P], U8, name="x_scale", align_bytes=64)
-        nc.vector.tensor_copy(x_scale[:], listed_scales[:].rearrange("p (h v d) -> p h d v", h=HALVES, d=D))
-
-        w_grouped = keep.tile([P, N, PACK], BF16, name="w_grouped", align_bytes=64)
-        nc.scalar.copy(w_grouped[:], w_raw[:].rearrange("p j n -> p n j"))
+        w_grouped = [keep.tile([P, P, PACK], BF16, name=f"w_grouped{mh}", align_bytes=64) for mh in range(2)]
         w_codes = keep.tile([P, N], U32, name="w_codes", align_bytes=64)
         w_scale = keep.tile([P, N], U8, name="w_scale", align_bytes=64)
-        nc.vector.quantize_mx(w_codes[:].bitcast(FP8X4), w_scale[:], w_grouped[:].rearrange("p n j -> p (n j)"))
+        for mh in range(2):
+            nc.scalar.copy(w_grouped[mh][:], w_raw[mh][:].rearrange("p j n -> p n j"))
 
-        y = []
-        for h in range(HALVES):
-            x_codes = keep.tile([P, D, P], U32, name=f"x_codes{h}", align_bytes=64)
+        def quantize(mh):
+            cols = slice(mh * P, (mh + 1) * P)
+            nc.vector.quantize_mx(
+                w_codes[:, cols].bitcast(FP8X4), w_scale[:, cols], w_grouped[mh][:].rearrange("p n j -> p (n j)")
+            )
+
+        listed_scales = keep.tile([P, S], U8, name="listed_scales", align_bytes=64)
+        x_scale = [keep.tile([P, D, P], U8, name=f"x_scale{h}", align_bytes=64) for h in range(HALVES)]
+        x_codes = [keep.tile([P, D, P], U32, name=f"x_codes{h}", align_bytes=64) for h in range(HALVES)]
+        y = [[psum.tile([P, 2, N], F32, name=f"y{h}{b}", tag=f"bank{h}{b}") for b in range(2)] for h in range(HALVES)]
+
+        def channel(h, d):
+            return y[h][d // 2][:, d % 2, :]
+
+        def deal_scales(h):
             nc.vector.tensor_copy(
-                x_codes[:].rearrange("p d v -> p v d"),
+                x_scale[h][:], listed_scales[:, h * D * P : (h + 1) * D * P].rearrange("p (v d) -> p d v", d=D)
+            )
+
+        def gather_words(h):
+            nc.vector.tensor_copy(
+                x_codes[h][:].rearrange("p d v -> p v d"),
                 word_table[:].indirect(offsets[:, 32 * h : 32 * (h + 1)]),
             )
-            banks = [psum.tile([P, 2, N], F32, name=f"y{h}{b}", tag=f"bank{h}{b}") for b in range(2)]
+
+        def multiply(h):
             for d in range(D):
                 nc.tensor.matmul_mx(
-                    banks[d // 2][:, d % 2, :],
-                    lhsT=x_codes[:, d, :].bitcast(FP8X4),
-                    lhsT_scale=x_scale[:, h, d, :],
+                    channel(h, d),
+                    lhsT=x_codes[h][:, d, :].bitcast(FP8X4),
+                    lhsT_scale=x_scale[h][:, d, :],
                     rhs=w_codes[:].bitcast(FP8X4),
                     rhs_scale=w_scale[:],
                     start=True,
                     stop=True,
                 )
-            y.append(banks)
+
+        nc.vector.tensor_copy(listed_scales[:], scale_table[:].indirect(offsets[:]))
+        quantize(0)
+        deal_scales(0)
+        quantize(1)
+        gather_words(0)
+        multiply(0)
+        deal_scales(1)
+        gather_words(1)
+        multiply(1)
 
         total = [[keep.tile([P, N], F32, name=f"total{h}{i}") for i in range(D)] for h in range(HALVES)]
         beam = [[keep.tile([P, N], F32, name=f"beam{h}{i}") for i in range(D)] for h in range(HALVES)]
         squares = [[keep.tile([P, 2, N], F32, name=f"squares{h}{b}") for b in range(2)] for h in range(HALVES)]
-        power_t = [psum.tile([P, 2, P], F32, name=f"power_t{h}") for h in range(HALVES)]
-        total_t = [psum.tile([P, 2, P], F32, name="total_t0")]
-        beam_t = [psum.tile([P, 2, P], F32, name="beam_t0")]
+        power_t = [[psum.tile([P, P], F32, name=f"power_t{h}{mh}") for mh in range(2)] for h in range(HALVES)]
         root = [keep.tile([P, 2, P], F32, name=f"root{h}") for h in range(HALVES)]
-        ratio = [keep.tile([P, 2, P], F32, name=f"ratio{h}") for h in range(HALVES)]
-        coherence = [keep.tile([P, 2, P], F32, name=f"coherence{h}") for h in range(HALVES)]
+        inverse = [keep.tile([P, 2, P], F32, name=f"inverse{h}") for h in range(HALVES)]
+        total_sq = [keep.tile([P, N], F32, name=f"total_sq{h}") for h in range(HALVES)]
+        numerator = [keep.tile([P, N], F32, name=f"numerator{h}") for h in range(HALVES)]
         result = [keep.tile([P, 2, P], F32, name=f"result{h}") for h in range(HALVES)]
+        halves = [slice(mh * P, (mh + 1) * P) for mh in range(2)]
+        whole = slice(0, N)
 
-        def channel(h, d):
-            return y[h][d // 2][:, d % 2, :]
+        def add_total(h, d, cols=whole):
+            nc.vector.tensor_tensor(total[h][d][:, cols], channel(h, d)[:, cols], total[h][d - 1][:, cols], ALU.add)
 
-        def open_sums(h):
-            nc.scalar.activation(total[h][0][:], channel(h, 0), ACT.Copy)
-            nc.scalar.activation(beam[h][0][:], channel(h, 0), ACT.Copy, scale=gain[:, h, 0:1])
-
-        def add_total(h, i, d):
-            nc.vector.tensor_tensor(total[h][i + 1][:], channel(h, d), total[h][i][:], ALU.add)
-
-        def add_beam(h, i, d):
+        def add_beam(h, d, cols=whole):
             nc.vector.scalar_tensor_tensor(
-                beam[h][i + 1][:], channel(h, d), gain[:, h, d : d + 1], beam[h][i][:], ALU.mult, ALU.add
+                beam[h][d][:, cols], channel(h, d)[:, cols], gain[:, h, d : d + 1], beam[h][d - 1][:, cols],
+                ALU.mult, ALU.add,
             )
 
         def square(h, b):
             nc.scalar.activation(squares[h][b][:], y[h][b][:], ACT.Square)
 
-        def turn_squares(h, order):
+        def turn_squares(h, b, first):
             for mh in range(2):
-                for i, d in enumerate(order):
+                for i in range(2):
                     nc.tensor.matmul(
-                        power_t[h][:, mh, :], squares[h][d // 2][:, d % 2, mh * P : (mh + 1) * P], identity[:],
-                        start=(i == 0), stop=(i == D - 1), is_transpose=True,
+                        power_t[h][mh][:], squares[h][b][:, i, halves[mh]], identity[:],
+                        start=(first and i == 0), stop=(not first and i == 1), is_transpose=True,
                     )
 
-        def turn(dst, src):
-            for mh in range(2):
-                nc.tensor.transpose(dst[:, mh, :], src[:, mh * P : (mh + 1) * P], identity[:])
-
         def find_root(h):
-            nc.scalar.activation(root[h][:], power_t[h][:], ACT.Abs_reciprocal_sqrt, bias=0.1, scale=4.0)
+            for mh in range(2):
+                nc.scalar.activation(root[h][:, mh, :], power_t[h][mh][:], ACT.Abs_reciprocal_sqrt, bias=0.1, scale=4.0)
 
-        def find_ratio(h):
-            nc.vector.tensor_tensor(ratio[h][:], total_t[h][:], root[h][:], ALU.mult)
+        def find_inverse(h):
+            nc.scalar.activation(inverse[h][:], root[h][:], ACT.Square)
 
-        def find_coherence(h):
-            nc.scalar.activation(coherence[h][:], ratio[h][:], ACT.Square)
-
-        def finish(h):
-            nc.vector.tensor_tensor(result[h][:], beam_t[h][:], coherence[h][:], ALU.mult)
+        def store(h):
             nc.sync.dma_start(out[:, h * P : (h + 1) * P].rearrange("(mh p) v -> p mh v", p=P), result[h][:])
 
-        open_sums(0)
-        square(0, 0)
-        for i, d in enumerate((2, 3, 1)):
-            add_total(0, i, d)
-            add_beam(0, i, d)
-        open_sums(1)
-        square(1, 1)
+        nc.vector.tensor_copy(total[0][0][:], channel(0, 0))
+        nc.vector.tensor_scalar(beam[0][0][:], channel(0, 0), gain[:, 0, 0:1], None, ALU.mult)
         square(0, 1)
-        turn(total_t[0], total[0][3])
-        turn(beam_t[0], beam[0][3])
-        turn_squares(0, (0, 1, 2, 3))
-        total_t.append(psum.tile([P, 2, P], F32, name="total_t1", tag="bank00"))
-        beam_t.append(psum.tile([P, 2, P], F32, name="beam_t1", tag="bank01"))
-        add_total(1, 0, 1)
-        add_beam(1, 0, 1)
+        add_total(0, 1)
+        add_beam(0, 1)
+        turn_squares(0, 1, True)
+        nc.scalar.activation(total[1][0][:], channel(1, 0), ACT.Copy)
+        nc.gpsimd.tensor_scalar(beam[1][0][:], total[1][0][:], gain[:, 1, 0:1], 0.0, ALU.mult, ALU.add)
         square(1, 0)
-        find_root(0)
-        add_total(1, 1, 2)
-        turn_squares(1, (2, 3, 0, 1))
-        find_ratio(0)
-        add_total(1, 2, 3)
+        add_total(0, 2)
+        add_beam(0, 2)
+        square(1, 1)
+        turn_squares(1, 0, True)
+        add_total(0, 3)
+        add_beam(0, 3)
+        square(0, 0)
+        turn_squares(1, 1, False)
+        nc.gpsimd.tensor_tensor(total_sq[0][:], total[0][3][:], total[0][3][:], ALU.mult)
+        add_total(1, 1)
+        add_beam(1, 1)
+        turn_squares(0, 0, False)
+        add_total(1, 2)
+        nc.gpsimd.tensor_tensor(numerator[0][:], total_sq[0][:], beam[0][3][:], ALU.mult)
         find_root(1)
-        find_coherence(0)
-        turn(total_t[1], total[1][3])
-        add_beam(1, 1, 2)
-        finish(0)
-        find_ratio(1)
-        add_beam(1, 2, 3)
-        find_coherence(1)
-        turn(beam_t[1], beam[1][3])
-        finish(1)
+        add_beam(1, 2)
+        for cols in halves:
+            add_total(1, 3, cols)
+        for cols in halves:
+            nc.scalar.activation(total_sq[1][:, cols], total[1][3][:, cols], ACT.Square)
+        for cols in halves:
+            add_beam(1, 3, cols)
+        find_root(0)
+        numerator_t0 = psum.tile([P, 2, P], F32, name="numerator_t0", tag="bank01")
+        for mh in range(2):
+            nc.tensor.transpose(numerator_t0[:, mh, :], numerator[0][:, halves[mh]], identity[:])
+        find_inverse(0)
+        numerator_t1 = [psum.tile([P, P], F32, name=f"numerator_t1{mh}", tag=f"bank{mh}0") for mh in range(2)]
+        for mh, cols in enumerate(halves):
+            nc.vector.tensor_tensor(numerator[1][:, cols], total_sq[1][:, cols], beam[1][3][:, cols], ALU.mult)
+            nc.tensor.transpose(numerator_t1[mh][:], numerator[1][:, cols], identity[:])
+        find_inverse(1)
+        nc.vector.tensor_tensor(result[0][:], numerator_t0[:], inverse[0][:], ALU.mult)
+        store(0)
+        for mh in range(2):
+            nc.vector.tensor_tensor(result[1][:, mh, :], numerator_t1[mh][:], inverse[1][:, mh, :], ALU.mult)
+        store(1)

@@ -31,19 +31,19 @@ def tile_picked_ydas_lin_p_kernel(tc, x_words, x_scales, w1, apo, offs, out):
         nc.sync.dma_start(offsets[:], offs)
 
         w_rows = w1.rearrange("(p j) n -> p j n", j=PACK)
-        w_raw = [keep.tile([P, PACK, P], F32, name=f"w_raw{mh}") for mh in range(2)]
-        nc.sync.dma_start(w_raw[0][:], w_rows[:, :, :P])
+        w_raw = keep.tile([P, PACK, N], F32, name="w_raw")
+        nc.sync.dma_start(w_raw[:, :2, :], w_rows[:, :2, :])
 
         scale_table = keep.tile([P, T], U8, name="scale_table", align_bytes=64)
         nc.vector.memset(scale_table[:].bitcast(I32), 0)
         for r in range(4):
-            (nc.sync, nc.scalar)[r % 2].dma_start(scale_table[r:P:32, :].bitcast(I32), x_scales[0, r:16:4, :].bitcast(I32))
+            nc.sync.dma_start(scale_table[r:P:32, :].bitcast(I32), x_scales[0, r:16:4, :].bitcast(I32))
         warm_in = keep.tile([P, 1], F32, name="warm_in")
         warm_out = keep.tile([P, 1], F32, name="warm_out")
         nc.vector.memset(warm_in[:], 1.0)
         nc.scalar.activation(warm_out[:], warm_in[:], ACT.Abs_reciprocal_sqrt)
 
-        nc.sync.dma_start(w_raw[1][:], w_rows[:, :, P:])
+        nc.sync.dma_start(w_raw[:, 2:, :], w_rows[:, 2:, :])
         word_table = keep.tile([P, T], U32, name="word_table", align_bytes=64)
         nc.sync.dma_start(word_table[:].bitcast(I32), x_words[0].rearrange("p n t -> p (n t)").bitcast(I32))
         gain = keep.tile([P, HALVES, D], F32, name="gain")
@@ -53,30 +53,26 @@ def tile_picked_ydas_lin_p_kernel(tc, x_words, x_scales, w1, apo, offs, out):
         nc.vector.memset(identity[:], 0.0)
         make_identity(nc, identity[:], nomemset=True)
 
-        w_grouped = [keep.tile([P, P, PACK], BF16, name=f"w_grouped{mh}", align_bytes=64) for mh in range(2)]
+        w_grouped = keep.tile([P, N, PACK], BF16, name="w_grouped", align_bytes=64)
         w_codes = keep.tile([P, N], U32, name="w_codes", align_bytes=64)
         w_scale = keep.tile([P, N], U8, name="w_scale", align_bytes=64)
-        for mh in range(2):
-            nc.scalar.copy(w_grouped[mh][:], w_raw[mh][:].rearrange("p j n -> p n j"))
-
-        def quantize(mh):
-            cols = slice(mh * P, (mh + 1) * P)
-            nc.vector.quantize_mx(
-                w_codes[:, cols].bitcast(FP8X4), w_scale[:, cols], w_grouped[mh][:].rearrange("p n j -> p (n j)")
-            )
+        nc.scalar.copy(w_grouped[:], w_raw[:].rearrange("p j n -> p n j"))
 
         listed_scales = keep.tile([P, S], U8, name="listed_scales", align_bytes=64)
-        x_scale = [keep.tile([P, D, P], U8, name=f"x_scale{h}", align_bytes=64) for h in range(HALVES)]
+        x_scale = {}
         x_codes = [keep.tile([P, D, P], U32, name=f"x_codes{h}", align_bytes=64) for h in range(HALVES)]
-        y = [[psum.tile([P, 2, N], F32, name=f"y{h}{b}", tag=f"bank{h}{b}") for b in range(2)] for h in range(HALVES)]
+        y_first = [psum.tile([P, N], F32, name=f"y0{d}", tag=f"bank{d}") for d in range(D)]
+        y_second = [psum.tile([P, 2, N], F32, name=f"y1{b}", tag=f"bank{4 + b}") for b in range(2)]
 
         def channel(h, d):
-            return y[h][d // 2][:, d % 2, :]
+            return y_second[d // 2][:, d % 2, :] if h else y_first[d][:]
 
-        def deal_scales(h):
-            nc.vector.tensor_copy(
-                x_scale[h][:], listed_scales[:, h * D * P : (h + 1) * D * P].rearrange("p (v d) -> p d v", d=D)
-            )
+        def deal_scales(h, first, count, tag):
+            dealt = keep.tile([P, count, P], U8, name=f"x_scale{h}{first}", tag=tag, align_bytes=64)
+            by_channel = listed_scales[:, h * D * P : (h + 1) * D * P].rearrange("p (v d) -> p d v", d=D)
+            nc.vector.tensor_copy(dealt[:], by_channel[:, first : first + count, :])
+            for i in range(count):
+                x_scale[h, first + i] = dealt[:, i, :]
 
         def gather_words(h):
             nc.vector.tensor_copy(
@@ -89,7 +85,7 @@ def tile_picked_ydas_lin_p_kernel(tc, x_words, x_scales, w1, apo, offs, out):
                 nc.tensor.matmul_mx(
                     channel(h, d),
                     lhsT=x_codes[h][:, d, :].bitcast(FP8X4),
-                    lhsT_scale=x_scale[h][:, d, :],
+                    lhsT_scale=x_scale[h, d],
                     rhs=w_codes[:].bitcast(FP8X4),
                     rhs_scale=w_scale[:],
                     start=True,
@@ -97,19 +93,19 @@ def tile_picked_ydas_lin_p_kernel(tc, x_words, x_scales, w1, apo, offs, out):
                 )
 
         nc.vector.tensor_copy(listed_scales[:], scale_table[:].indirect(offsets[:]))
-        quantize(0)
-        deal_scales(0)
-        quantize(1)
+        nc.vector.quantize_mx(w_codes[:].bitcast(FP8X4), w_scale[:], w_grouped[:].rearrange("p n j -> p (n j)"))
+        deal_scales(0, 0, 2, "shared_scales")
+        deal_scales(0, 2, 2, "own_scales")
         gather_words(0)
         multiply(0)
-        deal_scales(1)
         gather_words(1)
+        deal_scales(1, 0, D, "shared_scales")
         multiply(1)
 
         total = [[keep.tile([P, N], F32, name=f"total{h}{i}") for i in range(D)] for h in range(HALVES)]
         beam = [[keep.tile([P, N], F32, name=f"beam{h}{i}") for i in range(D)] for h in range(HALVES)]
-        squares = [[keep.tile([P, 2, N], F32, name=f"squares{h}{b}") for b in range(2)] for h in range(HALVES)]
-        power_t = [[psum.tile([P, P], F32, name=f"power_t{h}{mh}") for mh in range(2)] for h in range(HALVES)]
+        squares = [keep.tile([P, D, N], F32, name=f"squares{h}") for h in range(HALVES)]
+        power_t = [[psum.tile([P, P], F32, name=f"power_t0{mh}", tag=f"bank{6 + mh}") for mh in range(2)]]
         root = [keep.tile([P, 2, P], F32, name=f"root{h}") for h in range(HALVES)]
         inverse = [keep.tile([P, 2, P], F32, name=f"inverse{h}") for h in range(HALVES)]
         total_sq = [keep.tile([P, N], F32, name=f"total_sq{h}") for h in range(HALVES)]
@@ -127,20 +123,21 @@ def tile_picked_ydas_lin_p_kernel(tc, x_words, x_scales, w1, apo, offs, out):
                 ALU.mult, ALU.add,
             )
 
-        def square(h, b):
-            nc.scalar.activation(squares[h][b][:], y[h][b][:], ACT.Square)
+        def square_first(d):
+            nc.scalar.activation(squares[0][:, d, :], y_first[d][:], ACT.Square)
 
-        def turn_squares(h, b, first):
-            for mh in range(2):
-                for i in range(2):
-                    nc.tensor.matmul(
-                        power_t[h][mh][:], squares[h][b][:, i, halves[mh]], identity[:],
-                        start=(first and i == 0), stop=(not first and i == 1), is_transpose=True,
-                    )
+        def square_second(b):
+            nc.scalar.activation(squares[1][:, 2 * b : 2 * b + 2, :], y_second[b][:], ACT.Square)
 
-        def find_root(h):
-            for mh in range(2):
-                nc.scalar.activation(root[h][:, mh, :], power_t[h][mh][:], ACT.Abs_reciprocal_sqrt, bias=0.1, scale=4.0)
+        def turn_squares(h, mh, channels, opens=False, closes=False):
+            for d in channels:
+                nc.tensor.matmul(
+                    power_t[h][mh][:], squares[h][:, d, halves[mh]], identity[:],
+                    start=(opens and d == channels[0]), stop=(closes and d == channels[-1]), is_transpose=True,
+                )
+
+        def find_root(h, mh):
+            nc.scalar.activation(root[h][:, mh, :], power_t[h][mh][:], ACT.Abs_reciprocal_sqrt, bias=0.1, scale=4.0)
 
         def find_inverse(h):
             nc.scalar.activation(inverse[h][:], root[h][:], ACT.Square)
@@ -148,43 +145,51 @@ def tile_picked_ydas_lin_p_kernel(tc, x_words, x_scales, w1, apo, offs, out):
         def store(h):
             nc.sync.dma_start(out[:, h * P : (h + 1) * P].rearrange("(mh p) v -> p mh v", p=P), result[h][:])
 
-        nc.vector.tensor_copy(total[0][0][:], channel(0, 0))
-        nc.vector.tensor_scalar(beam[0][0][:], channel(0, 0), gain[:, 0, 0:1], None, ALU.mult)
-        square(0, 1)
+        nc.scalar.activation(total[0][0][:], channel(0, 0), ACT.Copy)
+        nc.scalar.activation(beam[0][0][:], channel(0, 0), ACT.Copy, scale=gain[:, 0, 0:1])
+        for d in (2, 3, 0):
+            square_first(d)
         add_total(0, 1)
         add_beam(0, 1)
-        turn_squares(0, 1, True)
+        for mh in range(2):
+            turn_squares(0, mh, (2, 3, 0), opens=True)
         nc.scalar.activation(total[1][0][:], channel(1, 0), ACT.Copy)
         nc.gpsimd.tensor_scalar(beam[1][0][:], total[1][0][:], gain[:, 1, 0:1], 0.0, ALU.mult, ALU.add)
-        square(1, 0)
+        square_second(0)
         add_total(0, 2)
         add_beam(0, 2)
-        square(1, 1)
-        turn_squares(1, 0, True)
+        square_second(1)
         add_total(0, 3)
         add_beam(0, 3)
-        square(0, 0)
-        turn_squares(1, 1, False)
+        power_t.append([psum.tile([P, P], F32, name=f"power_t1{mh}", tag=f"bank{3 * mh}") for mh in range(2)])
+        for mh in range(2):
+            turn_squares(1, mh, (0, 1), opens=True)
+        square_first(1)
+        turn_squares(1, 0, (2, 3), closes=True)
+        for mh in range(2):
+            turn_squares(0, mh, (1,), closes=True)
+        turn_squares(1, 1, (2, 3), closes=True)
         nc.gpsimd.tensor_tensor(total_sq[0][:], total[0][3][:], total[0][3][:], ALU.mult)
         add_total(1, 1)
         add_beam(1, 1)
-        turn_squares(0, 0, False)
         add_total(1, 2)
         nc.gpsimd.tensor_tensor(numerator[0][:], total_sq[0][:], beam[0][3][:], ALU.mult)
-        find_root(1)
+        find_root(1, 0)
+        find_root(0, 0)
+        find_root(0, 1)
+        find_root(1, 1)
         add_beam(1, 2)
         for cols in halves:
             add_total(1, 3, cols)
         for cols in halves:
-            nc.scalar.activation(total_sq[1][:, cols], total[1][3][:, cols], ACT.Square)
-        for cols in halves:
             add_beam(1, 3, cols)
-        find_root(0)
-        numerator_t0 = psum.tile([P, 2, P], F32, name="numerator_t0", tag="bank01")
+        for cols in halves:
+            nc.vector.tensor_tensor(total_sq[1][:, cols], total[1][3][:, cols], total[1][3][:, cols], ALU.mult)
+        numerator_t0 = psum.tile([P, 2, P], F32, name="numerator_t0", tag="bank2")
         for mh in range(2):
             nc.tensor.transpose(numerator_t0[:, mh, :], numerator[0][:, halves[mh]], identity[:])
         find_inverse(0)
-        numerator_t1 = [psum.tile([P, P], F32, name=f"numerator_t1{mh}", tag=f"bank{mh}0") for mh in range(2)]
+        numerator_t1 = [psum.tile([P, P], F32, name=f"numerator_t1{mh}", tag=f"bank{1 + 3 * mh}") for mh in range(2)]
         for mh, cols in enumerate(halves):
             nc.vector.tensor_tensor(numerator[1][:, cols], total_sq[1][:, cols], beam[1][3][:, cols], ALU.mult)
             nc.tensor.transpose(numerator_t1[mh][:], numerator[1][:, cols], identity[:])

from contextlib import ExitStack

import concourse.mybir as mybir
from concourse.masks import make_identity

K, T, S, D, N = 512, 2048, 1024, 4, 256
P = 128
PACK = 4
HALVES = S // (D * P)
FLOPS = 2 * K * N * S
BYTES = K * T + 16 * T + 4 * K * N + 4 * S + 2 * P * (S // 16) + 4 * N * (S // D)

F32 = mybir.dt.float32
BF16 = mybir.dt.bfloat16
I32 = mybir.dt.int32
U32 = mybir.dt.uint32
U16 = mybir.dt.uint16
U8 = mybir.dt.uint8
FP8X4 = mybir.dt.float8_e4m3fn_x4
ACT = mybir.ActivationFunctionType
ALU = mybir.AluOpType


def tile_picked_ydas_lin_p_kernel(tc, x_words, x_scales, w1, apo, offs, out):
    nc = tc.nc
    with ExitStack() as ctx:
        keep = ctx.enter_context(tc.tile_pool(name="keep", bufs=1))
        psum = ctx.enter_context(tc.psum_pool(name="psum", bufs=1))

        offsets = keep.tile([P, S // 16], U16, name="offsets")
        nc.sync.dma_start(offsets[:], offs)

        w_rows = w1.rearrange("(p j) n -> p j n", j=PACK)
        w_raw = keep.tile([P, PACK, N], F32, name="w_raw")
        nc.sync.dma_start(w_raw[:, :2, :], w_rows[:, :2, :])

        scale_table = keep.tile([P, T], U8, name="scale_table", align_bytes=64)
        nc.vector.memset(scale_table[:].bitcast(I32), 0)
        for r in range(4):
            nc.sync.dma_start(scale_table[r:P:32, :].bitcast(I32), x_scales[0, r:16:4, :].bitcast(I32))
        warm_in = keep.tile([P, 1], F32, name="warm_in")
        warm_out = keep.tile([P, 1], F32, name="warm_out")
        nc.vector.memset(warm_in[:], 1.0)
        nc.scalar.activation(warm_out[:], warm_in[:], ACT.Abs_reciprocal_sqrt)

        nc.sync.dma_start(w_raw[:, 2:, :], w_rows[:, 2:, :])
        word_table = keep.tile([P, T], U32, name="word_table", align_bytes=64)
        nc.sync.dma_start(word_table[:].bitcast(I32), x_words[0].rearrange("p n t -> p (n t)").bitcast(I32))
        gain = keep.tile([P, HALVES, D], F32, name="gain")
        nc.sync.dma_start(gain[:], apo[0, :].rearrange("(h v d) -> v h d", h=HALVES, d=D))

        identity = keep.tile([P, P], F32, name="identity")
        nc.vector.memset(identity[:], 0.0)
        make_identity(nc, identity[:], nomemset=True)

        w_grouped = keep.tile([P, N, PACK], BF16, name="w_grouped", align_bytes=64)
        w_codes = keep.tile([P, N], U32, name="w_codes", align_bytes=64)
        w_scale = keep.tile([P, N], U8, name="w_scale", align_bytes=64)
        nc.scalar.copy(w_grouped[:], w_raw[:].rearrange("p j n -> p n j"))

        listed_scales = keep.tile([P, S], U8, name="listed_scales", align_bytes=64)
        x_scale = {}
        x_codes = [keep.tile([P, D, P], U32, name=f"x_codes{h}", align_bytes=64) for h in range(HALVES)]
        y_first = [psum.tile([P, N], F32, name=f"y0{d}", tag=f"bank{d}") for d in range(D)]
        y_second = [psum.tile([P, 2, N], F32, name=f"y1{b}", tag=f"bank{4 + b}") for b in range(2)]

        def channel(h, d):
            return y_second[d // 2][:, d % 2, :] if h else y_first[d][:]

        def deal_scales(h, first, count, tag):
            dealt = keep.tile([P, count, P], U8, name=f"x_scale{h}{first}", tag=tag, align_bytes=64)
            by_channel = listed_scales[:, h * D * P : (h + 1) * D * P].rearrange("p (v d) -> p d v", d=D)
            nc.vector.tensor_copy(dealt[:], by_channel[:, first : first + count, :])
            for i in range(count):
                x_scale[h, first + i] = dealt[:, i, :]

        def gather_words(h):
            nc.vector.tensor_copy(
                x_codes[h][:].rearrange("p d v -> p v d"),
                word_table[:].indirect(offsets[:, 32 * h : 32 * (h + 1)]),
            )

        def multiply(h):
            for d in range(D):
                nc.tensor.matmul_mx(
                    channel(h, d),
                    lhsT=x_codes[h][:, d, :].bitcast(FP8X4),
                    lhsT_scale=x_scale[h, d],
                    rhs=w_codes[:].bitcast(FP8X4),
                    rhs_scale=w_scale[:],
                    start=True,
                    stop=True,
                )

        nc.vector.tensor_copy(listed_scales[:], scale_table[:].indirect(offsets[:]))
        nc.vector.quantize_mx(w_codes[:].bitcast(FP8X4), w_scale[:], w_grouped[:].rearrange("p n j -> p (n j)"))
        deal_scales(0, 0, 2, "shared_scales")
        deal_scales(0, 2, 2, "own_scales")
        gather_words(0)
        multiply(0)
        gather_words(1)
        deal_scales(1, 0, D, "shared_scales")
        multiply(1)

        total = [[keep.tile([P, N], F32, name=f"total{h}{i}") for i in range(D)] for h in range(HALVES)]
        beam = [[keep.tile([P, N], F32, name=f"beam{h}{i}") for i in range(D)] for h in range(HALVES)]
        squares = [keep.tile([P, D, N], F32, name=f"squares{h}") for h in range(HALVES)]
        power_t = [[psum.tile([P, P], F32, name=f"power_t0{mh}", tag=f"bank{6 + mh}") for mh in range(2)]]
        root = [keep.tile([P, 2, P], F32, name=f"root{h}") for h in range(HALVES)]
        inverse = [keep.tile([P, 2, P], F32, name=f"inverse{h}") for h in range(HALVES)]
        total_sq = [keep.tile([P, N], F32, name=f"total_sq{h}") for h in range(HALVES)]
        numerator = [keep.tile([P, N], F32, name=f"numerator{h}") for h in range(HALVES)]
        result = [keep.tile([P, 2, P], F32, name=f"result{h}") for h in range(HALVES)]
        halves = [slice(mh * P, (mh + 1) * P) for mh in range(2)]
        whole = slice(0, N)

        def add_total(h, d, cols=whole):
            nc.vector.tensor_tensor(total[h][d][:, cols], channel(h, d)[:, cols], total[h][d - 1][:, cols], ALU.add)

        def add_beam(h, d, cols=whole):
            nc.vector.scalar_tensor_tensor(
                beam[h][d][:, cols], channel(h, d)[:, cols], gain[:, h, d : d + 1], beam[h][d - 1][:, cols],
                ALU.mult, ALU.add,
            )

        def square_first(d):
            nc.scalar.activation(squares[0][:, d, :], y_first[d][:], ACT.Square)

        def square_second(b):
            nc.scalar.activation(squares[1][:, 2 * b : 2 * b + 2, :], y_second[b][:], ACT.Square)

        def turn_squares(h, mh, channels, opens=False, closes=False):
            for d in channels:
                nc.tensor.matmul(
                    power_t[h][mh][:], squares[h][:, d, halves[mh]], identity[:],
                    start=(opens and d == channels[0]), stop=(closes and d == channels[-1]), is_transpose=True,
                )

        def find_root(h, mh):
            nc.scalar.activation(root[h][:, mh, :], power_t[h][mh][:], ACT.Abs_reciprocal_sqrt, bias=0.1, scale=4.0)

        def find_inverse(h):
            nc.scalar.activation(inverse[h][:], root[h][:], ACT.Square)

        def store(h):
            nc.sync.dma_start(out[:, h * P : (h + 1) * P].rearrange("(mh p) v -> p mh v", p=P), result[h][:])

        nc.scalar.activation(total[0][0][:], channel(0, 0), ACT.Copy)
        nc.scalar.activation(beam[0][0][:], channel(0, 0), ACT.Copy, scale=gain[:, 0, 0:1])
        for d in (2, 3, 0):
            square_first(d)
        add_total(0, 1)
        add_beam(0, 1)
        for mh in range(2):
            turn_squares(0, mh, (2, 3, 0), opens=True)
        nc.scalar.activation(total[1][0][:], channel(1, 0), ACT.Copy)
        nc.gpsimd.tensor_scalar(beam[1][0][:], total[1][0][:], gain[:, 1, 0:1], 0.0, ALU.mult, ALU.add)
        square_second(0)
        add_total(0, 2)
        add_beam(0, 2)
        square_second(1)
        add_total(0, 3)
        add_beam(0, 3)
        power_t.append([psum.tile([P, P], F32, name=f"power_t1{mh}", tag=f"bank{3 * mh}") for mh in range(2)])
        for mh in range(2):
            turn_squares(1, mh, (0, 1), opens=True)
        square_first(1)
        turn_squares(1, 0, (2, 3), closes=True)
        for mh in range(2):
            turn_squares(0, mh, (1,), closes=True)
        turn_squares(1, 1, (2, 3), closes=True)
        nc.gpsimd.tensor_tensor(total_sq[0][:], total[0][3][:], total[0][3][:], ALU.mult)
        add_total(1, 1)
        add_beam(1, 1)
        add_total(1, 2)
        nc.gpsimd.tensor_tensor(numerator[0][:], total_sq[0][:], beam[0][3][:], ALU.mult)
        find_root(1, 0)
        find_root(0, 0)
        find_root(0, 1)
        find_root(1, 1)
        add_beam(1, 2)
        for cols in halves:
            add_total(1, 3, cols)
        for cols in halves:
            add_beam(1, 3, cols)
        for cols in halves:
            nc.vector.tensor_tensor(total_sq[1][:, cols], total[1][3][:, cols], total[1][3][:, cols], ALU.mult)
        numerator_t0 = psum.tile([P, 2, P], F32, name="numerator_t0", tag="bank2")
        for mh in range(2):
            nc.tensor.transpose(numerator_t0[:, mh, :], numerator[0][:, halves[mh]], identity[:])
        find_inverse(0)
        numerator_t1 = [psum.tile([P, P], F32, name=f"numerator_t1{mh}", tag=f"bank{1 + 3 * mh}") for mh in range(2)]
        for mh, cols in enumerate(halves):
            nc.vector.tensor_tensor(numerator[1][:, cols], total_sq[1][:, cols], beam[1][3][:, cols], ALU.mult)
            nc.tensor.transpose(numerator_t1[mh][:], numerator[1][:, cols], identity[:])
        find_inverse(1)
        nc.vector.tensor_tensor(result[0][:], numerator_t0[:], inverse[0][:], ALU.mult)
        store(0)
        for mh in range(2):
            nc.vector.tensor_tensor(result[1][:, mh, :], numerator_t1[mh][:], inverse[1][:, mh, :], ALU.mult)
        store(1)
